import numpy as np
import ml_dtypes


def mxq(x, axis, fmt="e4m3"):
    dtype, down = {"e4m3": (ml_dtypes.float8_e4m3fn, 7), "e5m2": (ml_dtypes.float8_e5m2, 14)}[fmt]
    v = np.moveaxis(np.asarray(x, np.float32).astype(ml_dtypes.bfloat16).astype(np.float64), axis, -1)
    blocks = v.reshape(v.shape[:-1] + (-1, 32))
    amax = np.abs(blocks).max(-1, keepdims=True)
    byte = np.maximum(np.where(amax > 0, np.frexp(amax)[1] - 1 + 127, 0) - down, 1)
    scale = np.exp2(byte - 127.0)
    codes = (blocks / scale).astype(np.float32).astype(dtype).astype(np.float64)
    return np.moveaxis((codes * scale).reshape(v.shape), -1, axis)


WIDE = False


def mx_kscale(k):
    if not WIDE:
        return np.ones(k)
    levels = np.array([10, -10, 5, -5, 0])
    if k % 512:
        return np.exp2(np.random.permutation(np.resize(levels, k // 32))).repeat(32)
    a = np.empty((k // 512, 16))
    for p in range(k // 512):
        a[p, :8] = np.random.permutation(np.resize(levels, 8))
        for g in range(8):
            far = levels[np.abs(levels - a[p, g]) >= 10]
            a[p, g + 8] = far[np.random.randint(len(far))]
    return np.exp2(a.ravel()).repeat(32)


def f64(x):
    return np.asarray(x).astype(np.float64)


def striped(idx):
    return np.tile(idx.reshape(-1, 16).T, (8, 1)).astype(np.uint16)


def unstriped(offs):
    return offs[:16].T.reshape(-1).astype(np.int64)


E2M1 = np.array([0.0, 0.5, 1.0, 1.5, 2.0, 3.0, 4.0, 6.0, -0.0, -0.5, -1.0, -1.5, -2.0, -3.0, -4.0, -6.0])


def pack_weight(w, fmt):
    k, n = w.shape
    w = f64(np.asarray(w, np.float32).astype(ml_dtypes.bfloat16)).reshape(k // 32, 32, n)
    amax = np.abs(w).max(1)
    if fmt == "e4m3":
        byte = np.frexp(amax)[1] - 1 + 127 - 7
    else:
        mant, ex = np.frexp(amax / 6.0)
        byte = np.where(mant > 0.5, ex, ex - 1) + 127
    byte = np.clip(np.where(amax > 0, byte, 1), 1, 254)
    scaled = (w * np.exp2(127.0 - byte)[:, None, :]).reshape(k, n).astype(np.float32)
    by_word = np.ascontiguousarray(scaled.reshape(k // 512, 128, 4, n).transpose(0, 1, 3, 2))
    if fmt == "e4m3":
        words = by_word.astype(ml_dtypes.float8_e4m3fn).view(np.uint8)
    else:
        c = by_word.astype(ml_dtypes.float4_e2m1fn).view(np.uint8) & 0xF
        words = (c[..., 0::2] | (c[..., 1::2] << 4)).reshape(k // 512, 128, 2 * n)
    return np.ascontiguousarray(words), np.ascontiguousarray(byte.astype(np.uint8).reshape(k // 512, 16, n))


def unpack_weight(words, scales, fmt):
    g, _, n = scales.shape
    words = np.ascontiguousarray(words).reshape(g, 128, n, -1)
    if fmt == "e4m3":
        vals = words.view(ml_dtypes.float8_e4m3fn).astype(np.float64)
    else:
        nib = np.empty((g, 128, n, 4), np.uint8)
        nib[..., 0::2] = words & 0xF
        nib[..., 1::2] = words >> 4
        vals = E2M1[nib]
    vals = vals * np.repeat(np.exp2(scales.astype(np.float64) - 127.0), 8, axis=1)[..., None]
    return vals.transpose(0, 1, 3, 2).reshape(g * 512, n)


def relu(v):
    return np.maximum(v, 0.0)


K, T, E, C, H, N = 1024, 512, 8, 128, 512, 384
TOP = 3
PAD = 64


def by_expert(wq, xq):
    return np.concatenate([wq[e].T @ xq[:, e * C:(e + 1) * C] for e in range(E)], axis=1)


def setup_inputs():
    n = np.random.standard_normal
    s = mx_kscale(K)[:, None]
    u = mx_kscale(H)
    slot_token = np.empty(E * C, np.int64); pos = np.tile(E * C + np.arange(T) % PAD, (TOP, 1)); taken = np.zeros(T, np.int64)
    liked = np.random.randn(T)
    for e in np.random.permutation(E):
        free = np.flatnonzero(taken < TOP); pick = np.random.permutation(free[np.argsort(-(liked[free] + np.random.gumbel(size=free.size)))[:C]]); slot_token[e * C:(e + 1) * C] = pick
        pos[taken[pick], pick] = e * C + np.arange(C); taken[pick] += 1
    g = np.random.uniform(0.2, 0.8, (TOP, T))
    w1 = [pack_weight(m, "e2m1") for m in n((E, K, H)) / np.sqrt(K) / s[None] * u[None, None, :]]
    w2 = [pack_weight(m, "e2m1") for m in n((E, H, N)) / np.sqrt(H) / u[None, :, None]]
    return {
        "xT": (n((K, T)) * s).astype(np.float32),
        "w1_words": np.stack([m[0] for m in w1]),
        "w1_scales": np.stack([m[1] for m in w1]),
        "w2_words": np.stack([m[0] for m in w2]),
        "w2_scales": np.stack([m[1] for m in w2]),
        "gate": np.stack([np.tile(r, (N, 1)) for r in g]).astype(np.float32),
        "offs": striped(slot_token),
        "pos1": striped(pos[0]),
        "pos2": striped(pos[1]),
        "pos3": striped(pos[2]),
    }


def reference(xT, w1_words, w1_scales, w2_words, w2_scales, gate, offs, pos1, pos2, pos3):
    idx = unstriped(offs)
    w1 = np.stack([unpack_weight(w1_words[e], w1_scales[e], "e2m1") for e in range(E)])
    w2 = np.stack([unpack_weight(w2_words[e], w2_scales[e], "e2m1") for e in range(E)])
    xq = mxq(f64(xT)[:, idx], 0, "e4m3")
    h = relu(by_expert(w1, xq))
    y = by_expert(w2, mxq(h, 0, "e4m3"))
    y = np.concatenate([y, np.zeros((N, PAD))], axis=1)
    return sum(f64(gate[r]) * y[:, unstriped(p)] for r, p in enumerate((pos1, pos2, pos3)))

@@ -1,0 +1,238 @@
+from contextlib import ExitStack
+
+import concourse.mybir as mybir
+from concourse.masks import make_identity
+
+K, T, E, C, H, N = 1024, 512, 8, 128, 512, 384
+TOP, PAD = 3, 64
+S = E * C
+P = 128
+PASSES = K // 512
+BLOCKS = N // P
+
+FLOPS = 2 * S * (K * H + H * N)
+BYTES = 4 * K * T + E * (K * H + H * N) * 17 // 32 + 4 * TOP * T + 2 * P * (S + TOP * T) // 16 + 4 * N * T
+
+F32 = mybir.dt.float32
+BF16 = mybir.dt.bfloat16
+I32 = mybir.dt.int32
+U32 = mybir.dt.uint32
+U16 = mybir.dt.uint16
+U8 = mybir.dt.uint8
+FP8X4 = mybir.dt.float8_e4m3fn_x4
+FP4X4 = mybir.dt.float4_e2m1fn_x4
+RELU = mybir.ActivationFunctionType.Relu
+MULT = mybir.AluOpType.mult
+ADD = mybir.AluOpType.add
+
+GROUPS = [(0, 1), (2, 3), (4, 5), (6,), (7,)]
+VECTOR_SHARE = 160
+HALF = T // 2
+
+
+def tile_moe_ecr_mlp_relu_kernel(tc, xT, w1_words, w1_scales, w2_words, w2_scales, gate, offs, pos1, pos2, pos3, out):
+    nc = tc.nc
+    with ExitStack() as ctx:
+        lists = ctx.enter_context(tc.tile_pool(name="lists", bufs=1))
+        keep = ctx.enter_context(tc.tile_pool(name="keep", bufs=1))
+        ring = ctx.enter_context(tc.tile_pool(name="ring", bufs=2))
+        acc_pool = ctx.enter_context(tc.psum_pool(name="acc", bufs=3))
+        turn_pool = ctx.enter_context(tc.psum_pool(name="turn", bufs=2))
+        y_pool = ctx.enter_context(tc.psum_pool(name="ybank", bufs=1))
+
+        w1_planes = [keep.tile([P, 4 * PASSES, H], U8, name=f"w1_plane{a}", align_bytes=64) for a in range(2)]
+        w2_plane = keep.tile([P, E, N], U8, name="w2_plane", align_bytes=64)
+        tok_words = [keep.tile([P, T], U32, name=f"tok_words{s}", align_bytes=64) for s in range(PASSES)]
+        tok_bytes = [keep.tile([P, T], U8, name=f"tok_bytes{s}", align_bytes=64) for s in range(PASSES)]
+        y_sb = [keep.tile([P, S + PAD], F32, name=f"y_sb{b}", align_bytes=64) for b in range(BLOCKS)]
+        ident = keep.tile([P, P], F32, name="ident", align_bytes=64)
+        for plane in w1_planes:
+            nc.vector.memset(plane[:].rearrange("p a i -> p (a i)").bitcast(I32), 0)
+        nc.gpsimd.memset(y_sb[0][:, S:], 0.0)
+        for s in range(PASSES):
+            nc.gpsimd.memset(tok_bytes[s][:].bitcast(I32), 0)
+        nc.gpsimd.memset(w2_plane[:].rearrange("p e n -> p (e n)").bitcast(I32), 0)
+        make_identity(nc, ident[:])
+        for b in range(1, BLOCKS):
+            nc.scalar.activation(y_sb[b][:, S:], y_sb[0][:, S:], RELU)
+
+        x_raw = {}
+
+        def load_x(s, h):
+            x_raw[s, h] = keep.tile([P, 4, HALF], F32, name=f"x_raw{s}{h}", align_bytes=64)
+            rows = xT[512 * s:512 * (s + 1), HALF * h:HALF * (h + 1)]
+            nc.sync.dma_start(x_raw[s, h][:], rows.rearrange("(p j) t -> p j t", j=4))
+
+        def load_list(name, src, entries):
+            t = lists.tile([P, entries // 16], U16, name=name)
+            nc.sync.dma_start(t[:], src)
+            return t
+
+        def load_scales(plane, src):
+            for r in range(4):
+                nc.sync.dma_start(plane[r:P:32, :, :].bitcast(I32), src[r].bitcast(I32))
+
+        w1_sb = {}
+
+        def load_w1(a):
+            w1_sb[a] = keep.tile([P, 2 * PASSES, 2 * H], U8, name=f"w1_sb{a}", align_bytes=64)
+            src = w1_words[2 * a:2 * a + 2].rearrange("e s p b -> p (e s) b")
+            nc.sync.dma_start(w1_sb[a][:].bitcast(I32), src.bitcast(I32))
+
+        def w1_rows(a):
+            return w1_scales[4 * a:4 * a + 4].rearrange("e s (q r) i -> r q (e s) i", r=4)
+
+        load_x(0, 0)
+        load_x(0, 1)
+        offs_sb = load_list("offs_sb", offs, S)
+        load_x(1, 0)
+        load_x(1, 1)
+        load_scales(w1_planes[0], w1_rows(0))
+        load_w1(0)
+        load_w1(1)
+        load_scales(w1_planes[1], w1_rows(1))
+        load_w1(2)
+        load_w1(3)
+        load_scales(w2_plane, w2_scales.rearrange("e s (q r) n -> r q (e s) n", r=4))
+        w2_sb = keep.tile([P, E, 2 * N], U8, name="w2_sb", align_bytes=64)
+        nc.sync.dma_start(w2_sb[:].bitcast(I32), w2_words.rearrange("e s p b -> p (e s) b").bitcast(I32))
+        pos_sb = [load_list(f"pos_sb{r}", src, T) for r, src in enumerate((pos1, pos2, pos3))]
+        gate_sb = keep.tile([P, TOP, T], F32, name="gate_sb", align_bytes=64)
+        nc.sync.dma_start(gate_sb[:], gate[:, 0:P, :].rearrange("r p t -> p r t"))
+
+        def quantise_tokens(s, h, vector_tokens):
+            x_bf = keep.tile([P, HALF, 4], BF16, name=f"x_bf{s}{h}", align_bytes=64)
+            for move, lo, hi in ((nc.vector.tensor_copy, 0, vector_tokens), (nc.scalar.copy, vector_tokens, HALF)):
+                if lo < hi:
+                    move(x_bf[:, lo:hi, :].rearrange("p (c i) j -> p c j i", i=4),
+                         x_raw[s, h][:, :, lo:hi].rearrange("p j (c i) -> p c j i", i=4))
+            cols = slice(HALF * h, HALF * (h + 1))
+            nc.vector.quantize_mx(out=tok_words[s][:, cols].bitcast(FP8X4), scales=tok_bytes[s][:, cols],
+                                  in_=x_bf[:].rearrange("p t j -> p (t j)"))
+
+        slot_words = {}
+        slot_bytes = {}
+        h_words = {}
+        h_bytes = {}
+
+        def gather(s, pair, cuts):
+            words = ring.tile([P, 2 * C], U32, name=f"slot_words{s}", align_bytes=64)
+            scale = ring.tile([P, 2 * C], U8, name=f"slot_bytes{s}", align_bytes=64)
+            n = 2 * C // cuts
+            for a in range(cuts):
+                first = 2 * C * pair + n * a
+                idx = offs_sb[:, first // 16:(first + n) // 16]
+                nc.vector.tensor_copy(words[:, n * a:n * (a + 1)], tok_words[s][:].indirect(idx))
+                nc.vector.tensor_copy(scale[:, n * a:n * (a + 1)], tok_bytes[s][:].indirect(idx))
+            for g in range(2):
+                slot_words[2 * pair + g, s] = words[:, C * g:C * (g + 1)]
+                slot_bytes[2 * pair + g, s] = scale[:, C * g:C * (g + 1)]
+
+        def first_layer(group):
+            n = len(group)
+            turned = turn_pool.tile([P, n, 2, C], F32, name="turned")
+            for g, e in enumerate(group):
+                acc = acc_pool.tile([P, H], F32, name="acc")
+                for s in range(PASSES):
+                    nc.tensor.matmul_mx(acc[:], lhsT=slot_words[e, s].bitcast(FP8X4), lhsT_scale=slot_bytes[e, s],
+                                        rhs=w1_sb[e // 2][:, PASSES * (e % 2) + s, :].bitcast(FP4X4),
+                                        rhs_scale=w1_planes[e // 4][:, PASSES * (e % 4) + s, :],
+                                        start=(s == 0), stop=(s == PASSES - 1))
+                h_rows = keep.tile([P, H], BF16, name=f"h_rows{e}", align_bytes=64)
+                dst = h_rows[:].rearrange("m (u p d) -> m u p d", u=2, d=2)
+                src = acc[:].rearrange("m (p u d) -> m u p d", u=2, d=2)
+                if e == E - 1:
+                    nc.vector.tensor_scalar_max(dst, src, 0.0)
+                else:
+                    nc.scalar.activation(dst, src, RELU)
+                pairs = h_rows[:].bitcast(F32)
+                for u in range(2):
+                    nc.tensor.transpose(turned[:, g, u, :], pairs[:, P * u:P * (u + 1)], ident[:])
+            h_bf = keep.tile([P, 4 * C * n], BF16, name=f"h_bf{group[0]}", align_bytes=64)
+            nc.scalar.copy(h_bf[:].bitcast(F32).rearrange("p (g m u) -> p g m u", g=n, u=2),
+                           turned[:].rearrange("p g u m -> p g m u"))
+            words = keep.tile([P, C * n], U32, name=f"h_words{group[0]}", align_bytes=64)
+            scale = keep.tile([P, C * n], U8, name=f"h_bytes{group[0]}", align_bytes=64)
+            nc.vector.quantize_mx(out=words[:].bitcast(FP8X4), scales=scale[:], in_=h_bf[:])
+            for g, e in enumerate(group):
+                h_words[e] = words[:, C * g:C * (g + 1)]
+                h_bytes[e] = scale[:, C * g:C * (g + 1)]
+
+        def second_layer(b, experts, tag, move):
+            bank = y_pool.tile([P, C * len(experts)], F32, name=tag)
+            for g, e in enumerate(experts):
+                nc.tensor.matmul_mx(bank[:, C * g:C * (g + 1)],
+                                    lhsT=w2_sb[:, e, 2 * P * b:2 * P * (b + 1)].bitcast(FP4X4),
+                                    lhsT_scale=w2_plane[:, e, P * b:P * (b + 1)],
+                                    rhs=h_words[e].bitcast(FP8X4), rhs_scale=h_bytes[e], start=True, stop=True)
+            move(y_sb[b][:, C * experts[0]:C * (experts[-1] + 1)], bank[:])
+
+        quantise_tokens(0, 0, HALF)
+        quantise_tokens(0, 1, VECTOR_SHARE)
+        gather(0, 0, 1)
+        gather(0, 1, 1)
+        for h in range(2):
+            quantise_tokens(1, h, 0)
+        for group in GROUPS:
+            if group[0] in (4, 6):
+                gather(0, group[0] // 2, 1)
+            if group[0] % 2 == 0:
+                gather(1, group[0] // 2, 2 if group[0] == 6 else 1)
+            first_layer(group)
+        second_layer(0, (0, 1, 2, 3), "bank_a", nc.scalar.copy)
+        second_layer(0, (4, 5, 6), "bank_b", nc.vector.tensor_copy)
+        second_layer(0, (7,), "bank_c", nc.scalar.copy)
+        for b in range(1, BLOCKS):
+            second_layer(b, (0, 1, 2, 3), "bank_c", nc.scalar.copy)
+            second_layer(b, (4, 5, 6, 7), "bank_a" if b == 1 else "bank_b", nc.scalar.copy)
+
+        def fetch(b, r, tag, lo=0, hi=T):
+            term = keep.tile([P, hi - lo], F32, name=tag, align_bytes=64)
+            nc.vector.tensor_tensor(term[:], y_sb[b][:].indirect(pos_sb[r][:, lo // 16:hi // 16]), gate_sb[:, r, lo:hi], MULT)
+            return term
+
+        def turned_sum(b, choices, sums, backs):
+            width = T // len(sums)
+            per = width // P
+            for r in range(choices):
+                cuts = len(sums) if r == choices - 1 else 1
+                for a in range(cuts):
+                    lo = T // cuts * a
+                    term = fetch(b, r, f"term{b}{r}{a}", lo, lo + T // cuts)
+                    for q in range(lo // P, (lo + T // cuts) // P):
+                        nc.tensor.matmul(sums[q // per][:, P * (q % per):P * (q % per + 1)],
+                                         lhsT=term[:, P * q - lo:P * (q + 1) - lo],
+                                         rhs=ident[:], is_transpose=True, start=(r == 0 and q % per == 0),
+                                         stop=(r == choices - 1 and q % per == per - 1))
+            for a, (summed, back) in enumerate(zip(sums, backs)):
+                summed_sb = keep.tile([P, width], F32, name=f"summed_sb{b}{a}", align_bytes=64)
+                nc.scalar.copy(summed_sb[:], summed[:])
+                for q in range(per):
+                    cols = slice(P * q, P * (q + 1))
+                    nc.tensor.transpose(back[:, cols], summed_sb[:, cols], ident[:])
+
+        def copy_and_store(b, backs):
+            width = T // len(backs)
+            for a, back in enumerate(backs):
+                result = keep.tile([P, width], F32, name=f"result{b}{a}", align_bytes=64)
+                nc.scalar.copy(result[:], back[:])
+                nc.sync.dma_start(out[P * b:P * (b + 1), width * a:width * (a + 1)], result[:])
+
+        backs = [turn_pool.tile([P, T], F32, name="turned")]
+        turned_sum(0, TOP, [acc_pool.tile([P, T], F32, name="acc")], backs)
+        copy_and_store(0, backs)
+
+        partial = turn_pool.tile([P, T], F32, name="turned")
+        turned_sum(1, TOP - 1, [acc_pool.tile([P, T], F32, name="acc")], [partial])
+
+        sums = [acc_pool.tile([P, HALF], F32, name="acc"), y_pool.tile([P, HALF], F32, name="bank_a")]
+        backs = [y_pool.tile([P, HALF], F32, name="bank_b"), y_pool.tile([P, HALF], F32, name="bank_c")]
+        turned_sum(2, TOP, sums, backs)
+        copy_and_store(2, backs)
+
+        for a in range(2):
+            lo, hi = HALF * a, HALF * (a + 1)
+            last = fetch(1, TOP - 1, f"term1{a}0", lo, hi)
+            result = keep.tile([P, HALF], F32, name=f"result1{a}", align_bytes=64)
+            nc.vector.tensor_tensor(result[:], partial[:, lo:hi], last[:], ADD)
+            nc.sync.dma_start(out[P:2 * P, lo:hi], result[:])

@@ -25,7 +25,6 @@ RELU = mybir.ActivationFunctionType.Relu
 MULT = mybir.AluOpType.mult
 ADD = mybir.AluOpType.add
 
-GROUPS = [(0, 1), (2, 3), (4, 5), (6,), (7,)]
 VECTOR_SHARE = 160
 HALF = T // 2
 
@@ -35,10 +34,7 @@ def tile_moe_ecr_mlp_relu_kernel(tc, xT, w1_words, w1_scales, w2_words, w2_scale
     with ExitStack() as ctx:
         lists = ctx.enter_context(tc.tile_pool(name="lists", bufs=1))
         keep = ctx.enter_context(tc.tile_pool(name="keep", bufs=1))
-        ring = ctx.enter_context(tc.tile_pool(name="ring", bufs=2))
-        acc_pool = ctx.enter_context(tc.psum_pool(name="acc", bufs=3))
-        turn_pool = ctx.enter_context(tc.psum_pool(name="turn", bufs=2))
-        y_pool = ctx.enter_context(tc.psum_pool(name="ybank", bufs=1))
+        psum = ctx.enter_context(tc.psum_pool(name="psum", bufs=1))
 
         w1_planes = [keep.tile([P, 4 * PASSES, H], U8, name=f"w1_plane{a}", align_bytes=64) for a in range(2)]
         w2_plane = keep.tile([P, E, N], U8, name="w2_plane", align_bytes=64)
@@ -89,10 +85,9 @@ def tile_moe_ecr_mlp_relu_kernel(tc, xT, w1_words, w1_scales, w2_words, w2_scale
         load_x(1, 1)
         load_scales(w1_planes[0], w1_rows(0))
         load_w1(0)
-        load_w1(1)
         load_scales(w1_planes[1], w1_rows(1))
-        load_w1(2)
-        load_w1(3)
+        for a in range(1, E // 2):
+            load_w1(a)
         load_scales(w2_plane, w2_scales.rearrange("e s (q r) n -> r q (e s) n", r=4))
         w2_sb = keep.tile([P, E, 2 * N], U8, name="w2_sb", align_bytes=64)
         nc.sync.dma_start(w2_sb[:].bitcast(I32), w2_words.rearrange("e s p b -> p (e s) b").bitcast(I32))
@@ -115,42 +110,51 @@ def tile_moe_ecr_mlp_relu_kernel(tc, xT, w1_words, w1_scales, w2_words, w2_scale
         h_words = {}
         h_bytes = {}
 
-        def gather(s, pair, cuts):
-            words = ring.tile([P, 2 * C], U32, name=f"slot_words{s}", align_bytes=64)
-            scale = ring.tile([P, 2 * C], U8, name=f"slot_bytes{s}", align_bytes=64)
-            n = 2 * C // cuts
-            for a in range(cuts):
-                first = 2 * C * pair + n * a
-                idx = offs_sb[:, first // 16:(first + n) // 16]
-                nc.vector.tensor_copy(words[:, n * a:n * (a + 1)], tok_words[s][:].indirect(idx))
-                nc.vector.tensor_copy(scale[:, n * a:n * (a + 1)], tok_bytes[s][:].indirect(idx))
-            for g in range(2):
-                slot_words[2 * pair + g, s] = words[:, C * g:C * (g + 1)]
-                slot_bytes[2 * pair + g, s] = scale[:, C * g:C * (g + 1)]
+        def gather(s, cuts, tag):
+            first = cuts[0][0]
+            width = C * sum(len(cut) for cut in cuts)
+            words = keep.tile([P, width], U32, name="slot_words" + tag, align_bytes=64)
+            scale = keep.tile([P, width], U8, name="slot_bytes" + tag, align_bytes=64)
+            for cut in cuts:
+                idx = offs_sb[:, C * cut[0] // 16:C * (cut[-1] + 1) // 16]
+                cols = slice(C * (cut[0] - first), C * (cut[-1] + 1 - first))
+                nc.vector.tensor_copy(words[:, cols], tok_words[s][:].indirect(idx))
+                nc.vector.tensor_copy(scale[:, cols], tok_bytes[s][:].indirect(idx))
+                for e in cut:
+                    cols = slice(C * (e - first), C * (e + 1 - first))
+                    slot_words[e, s] = words[:, cols]
+                    slot_bytes[e, s] = scale[:, cols]
 
-        def first_layer(group):
+        def bank(number, shape):
+            return psum.tile(shape, F32, name=f"bank{number}")
+
+        h_rows = {}
+
+        def first_layer(e, number):
+            acc = bank(number, [P, H])
+            for s in range(PASSES):
+                nc.tensor.matmul_mx(acc[:], lhsT=slot_words[e, s].bitcast(FP8X4), lhsT_scale=slot_bytes[e, s],
+                                    rhs=w1_sb[e // 2][:, PASSES * (e % 2) + s, :].bitcast(FP4X4),
+                                    rhs_scale=w1_planes[e // 4][:, PASSES * (e % 4) + s, :],
+                                    start=(s == 0), stop=(s == PASSES - 1))
+            h_rows[e] = keep.tile([P, H], BF16, name=f"h_rows{e}", align_bytes=64)
+            dst = h_rows[e][:].rearrange("m (u p d) -> m u p d", u=2, d=2)
+            src = acc[:].rearrange("m (p u d) -> m u p d", u=2, d=2)
+            if e == E - 1:
+                nc.vector.tensor_scalar_max(dst, src, 0.0)
+            else:
+                nc.scalar.activation(dst, src, RELU)
+
+        def quantise_hidden(group, number, move):
             n = len(group)
-            turned = turn_pool.tile([P, n, 2, C], F32, name="turned")
+            turned = bank(number, [P, n, 2, C])
             for g, e in enumerate(group):
-                acc = acc_pool.tile([P, H], F32, name="acc")
-                for s in range(PASSES):
-                    nc.tensor.matmul_mx(acc[:], lhsT=slot_words[e, s].bitcast(FP8X4), lhsT_scale=slot_bytes[e, s],
-                                        rhs=w1_sb[e // 2][:, PASSES * (e % 2) + s, :].bitcast(FP4X4),
-                                        rhs_scale=w1_planes[e // 4][:, PASSES * (e % 4) + s, :],
-                                        start=(s == 0), stop=(s == PASSES - 1))
-                h_rows = keep.tile([P, H], BF16, name=f"h_rows{e}", align_bytes=64)
-                dst = h_rows[:].rearrange("m (u p d) -> m u p d", u=2, d=2)
-                src = acc[:].rearrange("m (p u d) -> m u p d", u=2, d=2)
-                if e == E - 1:
-                    nc.vector.tensor_scalar_max(dst, src, 0.0)
-                else:
-                    nc.scalar.activation(dst, src, RELU)
-                pairs = h_rows[:].bitcast(F32)
+                pairs = h_rows[e][:].bitcast(F32)
                 for u in range(2):
                     nc.tensor.transpose(turned[:, g, u, :], pairs[:, P * u:P * (u + 1)], ident[:])
             h_bf = keep.tile([P, 4 * C * n], BF16, name=f"h_bf{group[0]}", align_bytes=64)
-            nc.scalar.copy(h_bf[:].bitcast(F32).rearrange("p (g m u) -> p g m u", g=n, u=2),
-                           turned[:].rearrange("p g u m -> p g m u"))
+            move(h_bf[:].bitcast(F32).rearrange("p (g m u) -> p g m u", g=n, u=2),
+                 turned[:].rearrange("p g u m -> p g m u"))
             words = keep.tile([P, C * n], U32, name=f"h_words{group[0]}", align_bytes=64)
             scale = keep.tile([P, C * n], U8, name=f"h_bytes{group[0]}", align_bytes=64)
             nc.vector.quantize_mx(out=words[:].bitcast(FP8X4), scales=scale[:], in_=h_bf[:])
@@ -158,33 +162,46 @@ def tile_moe_ecr_mlp_relu_kernel(tc, xT, w1_words, w1_scales, w2_words, w2_scale
                 h_words[e] = words[:, C * g:C * (g + 1)]
                 h_bytes[e] = scale[:, C * g:C * (g + 1)]
 
-        def second_layer(b, experts, tag, move):
-            bank = y_pool.tile([P, C * len(experts)], F32, name=tag)
+        def second_layer(b, experts, number, move):
+            y_ps = bank(number, [P, C * len(experts)])
             for g, e in enumerate(experts):
-                nc.tensor.matmul_mx(bank[:, C * g:C * (g + 1)],
+                nc.tensor.matmul_mx(y_ps[:, C * g:C * (g + 1)],
                                     lhsT=w2_sb[:, e, 2 * P * b:2 * P * (b + 1)].bitcast(FP4X4),
                                     lhsT_scale=w2_plane[:, e, P * b:P * (b + 1)],
                                     rhs=h_words[e].bitcast(FP8X4), rhs_scale=h_bytes[e], start=True, stop=True)
-            move(y_sb[b][:, C * experts[0]:C * (experts[-1] + 1)], bank[:])
+            move(y_sb[b][:, C * experts[0]:C * (experts[-1] + 1)], y_ps[:])
 
         quantise_tokens(0, 0, HALF)
         quantise_tokens(0, 1, VECTOR_SHARE)
-        gather(0, 0, 1)
-        gather(0, 1, 1)
+        gather(0, [(0, 1)], "_a")
+        gather(0, [(2, 3)], "_b")
         for h in range(2):
             quantise_tokens(1, h, 0)
-        for group in GROUPS:
-            if group[0] in (4, 6):
-                gather(0, group[0] // 2, 1)
-            if group[0] % 2 == 0:
-                gather(1, group[0] // 2, 2 if group[0] == 6 else 1)
-            first_layer(group)
-        second_layer(0, (0, 1, 2, 3), "bank_a", nc.scalar.copy)
-        second_layer(0, (4, 5, 6), "bank_b", nc.vector.tensor_copy)
-        second_layer(0, (7,), "bank_c", nc.scalar.copy)
+        gather(1, [(0,), (1,)], "_c")
+        gather(1, [(2, 3)], "_d")
+        first_layer(0, 0)
+        first_layer(1, 1)
+        gather(1, [(4, 5)], "_c")
+        gather(0, [(4, 5)], "_a")
+        first_layer(2, 2)
+        first_layer(3, 3)
+        gather(0, [(6, 7)], "_b")
+        gather(1, [(6,), (7,)], "_d")
+        quantise_hidden((0, 1), 2, nc.scalar.copy)
+        first_layer(4, 0)
+        first_layer(5, 1)
+        quantise_hidden((2, 3), 0, nc.scalar.copy)
+        first_layer(6, 3)
+        first_layer(7, 4)
+        quantise_hidden((4, 5), 3, nc.scalar.copy)
+        quantise_hidden((6,), 1, nc.vector.tensor_copy)
+        quantise_hidden((7,), 2, nc.scalar.copy)
+        second_layer(0, (0, 1, 2, 3), 5, nc.scalar.copy)
+        second_layer(0, (4, 5), 6, nc.vector.tensor_copy)
+        second_layer(0, (6, 7), 7, nc.scalar.copy)
         for b in range(1, BLOCKS):
-            second_layer(b, (0, 1, 2, 3), "bank_c", nc.scalar.copy)
-            second_layer(b, (4, 5, 6, 7), "bank_a" if b == 1 else "bank_b", nc.scalar.copy)
+            second_layer(b, (0, 1, 2, 3), 7, nc.scalar.copy)
+            second_layer(b, (4, 5, 6, 7), 5 if b == 1 else 6, nc.scalar.copy)
 
         def fetch(b, r, tag, lo=0, hi=T):
             term = keep.tile([P, hi - lo], F32, name=tag, align_bytes=64)
@@ -218,15 +235,15 @@ def tile_moe_ecr_mlp_relu_kernel(tc, xT, w1_words, w1_scales, w2_words, w2_scale
                 nc.scalar.copy(result[:], back[:])
                 nc.sync.dma_start(out[P * b:P * (b + 1), width * a:width * (a + 1)], result[:])
 
-        backs = [turn_pool.tile([P, T], F32, name="turned")]
-        turned_sum(0, TOP, [acc_pool.tile([P, T], F32, name="acc")], backs)
+        backs = [bank(1, [P, T])]
+        turned_sum(0, TOP, [bank(0, [P, T])], backs)
         copy_and_store(0, backs)
 
-        partial = turn_pool.tile([P, T], F32, name="turned")
-        turned_sum(1, TOP - 1, [acc_pool.tile([P, T], F32, name="acc")], [partial])
+        partial = bank(3, [P, T])
+        turned_sum(1, TOP - 1, [bank(2, [P, T])], [partial])
 
-        sums = [acc_pool.tile([P, HALF], F32, name="acc"), y_pool.tile([P, HALF], F32, name="bank_a")]
-        backs = [y_pool.tile([P, HALF], F32, name="bank_b"), y_pool.tile([P, HALF], F32, name="bank_c")]
+        sums = [bank(4, [P, HALF]), bank(5, [P, HALF])]
+        backs = [bank(6, [P, HALF]), bank(7, [P, HALF])]
         turned_sum(2, TOP, sums, backs)
         copy_and_store(2, backs)
 

@@ -42,12 +42,12 @@ def tile_moe_ecr_mlp_relu_kernel(tc, xT, w1_words, w1_scales, w2_words, w2_scale
         tok_bytes = [keep.tile([P, T], U8, name=f"tok_bytes{s}", align_bytes=64) for s in range(PASSES)]
         y_sb = [keep.tile([P, S + PAD], F32, name=f"y_sb{b}", align_bytes=64) for b in range(BLOCKS)]
         ident = keep.tile([P, P], F32, name="ident", align_bytes=64)
+        nc.vector.memset(y_sb[0][:, S:], 0.0)
         for plane in w1_planes:
             nc.vector.memset(plane[:].rearrange("p a i -> p (a i)").bitcast(I32), 0)
-        nc.gpsimd.memset(y_sb[0][:, S:], 0.0)
         for s in range(PASSES):
-            nc.gpsimd.memset(tok_bytes[s][:].bitcast(I32), 0)
-        nc.gpsimd.memset(w2_plane[:].rearrange("p e n -> p (e n)").bitcast(I32), 0)
+            nc.vector.memset(tok_bytes[s][:].bitcast(I32), 0)
+        nc.vector.memset(w2_plane[:].rearrange("p e n -> p (e n)").bitcast(I32), 0)
         make_identity(nc, ident[:])
         for b in range(1, BLOCKS):
             nc.scalar.activation(y_sb[b][:, S:], y_sb[0][:, S:], RELU)
@@ -85,9 +85,10 @@ def tile_moe_ecr_mlp_relu_kernel(tc, xT, w1_words, w1_scales, w2_words, w2_scale
         load_x(1, 1)
         load_scales(w1_planes[0], w1_rows(0))
         load_w1(0)
+        load_w1(1)
         load_scales(w1_planes[1], w1_rows(1))
-        for a in range(1, E // 2):
-            load_w1(a)
+        load_w1(2)
+        load_w1(3)
         load_scales(w2_plane, w2_scales.rearrange("e s (q r) n -> r q (e s) n", r=4))
         w2_sb = keep.tile([P, E, 2 * N], U8, name="w2_sb", align_bytes=64)
         nc.sync.dma_start(w2_sb[:].bitcast(I32), w2_words.rearrange("e s p b -> p (e s) b").bitcast(I32))
@@ -179,9 +180,9 @@ def tile_moe_ecr_mlp_relu_kernel(tc, xT, w1_words, w1_scales, w2_words, w2_scale
             quantise_tokens(1, h, 0)
         gather(1, [(0,), (1,)], "_c")
         gather(1, [(2, 3)], "_d")
+        gather(1, [(4, 5)], "_e")
         first_layer(0, 0)
         first_layer(1, 1)
-        gather(1, [(4, 5)], "_c")
         gather(0, [(4, 5)], "_a")
         first_layer(2, 2)
         first_layer(3, 3)

@@ -42,12 +42,12 @@ def tile_moe_ecr_mlp_relu_kernel(tc, xT, w1_words, w1_scales, w2_words, w2_scale
         tok_bytes = [keep.tile([P, T], U8, name=f"tok_bytes{s}", align_bytes=64) for s in range(PASSES)]
         y_sb = [keep.tile([P, S + PAD], F32, name=f"y_sb{b}", align_bytes=64) for b in range(BLOCKS)]
         ident = keep.tile([P, P], F32, name="ident", align_bytes=64)
-        nc.vector.memset(y_sb[0][:, S:], 0.0)
         for plane in w1_planes:
             nc.vector.memset(plane[:].rearrange("p a i -> p (a i)").bitcast(I32), 0)
+        nc.gpsimd.memset(y_sb[0][:, S:], 0.0)
         for s in range(PASSES):
-            nc.vector.memset(tok_bytes[s][:].bitcast(I32), 0)
-        nc.vector.memset(w2_plane[:].rearrange("p e n -> p (e n)").bitcast(I32), 0)
+            nc.gpsimd.memset(tok_bytes[s][:].bitcast(I32), 0)
+        nc.gpsimd.memset(w2_plane[:].rearrange("p e n -> p (e n)").bitcast(I32), 0)
         make_identity(nc, ident[:])
         for b in range(1, BLOCKS):
             nc.scalar.activation(y_sb[b][:, S:], y_sb[0][:, S:], RELU)
@@ -131,20 +131,22 @@ def tile_moe_ecr_mlp_relu_kernel(tc, xT, w1_words, w1_scales, w2_words, w2_scale
 
         h_rows = {}
 
-        def first_layer(e, number):
-            acc = bank(number, [P, H])
-            for s in range(PASSES):
-                nc.tensor.matmul_mx(acc[:], lhsT=slot_words[e, s].bitcast(FP8X4), lhsT_scale=slot_bytes[e, s],
-                                    rhs=w1_sb[e // 2][:, PASSES * (e % 2) + s, :].bitcast(FP4X4),
-                                    rhs_scale=w1_planes[e // 4][:, PASSES * (e % 4) + s, :],
-                                    start=(s == 0), stop=(s == PASSES - 1))
-            h_rows[e] = keep.tile([P, H], BF16, name=f"h_rows{e}", align_bytes=64)
-            dst = h_rows[e][:].rearrange("m (u p d) -> m u p d", u=2, d=2)
-            src = acc[:].rearrange("m (p u d) -> m u p d", u=2, d=2)
-            if e == E - 1:
-                nc.vector.tensor_scalar_max(dst, src, 0.0)
-            else:
-                nc.scalar.activation(dst, src, RELU)
+        def first_layer(pair, numbers, passes):
+            accs = [bank(number, [P, H]) for number in numbers]
+            for s in passes:
+                for e, acc in zip(pair, accs):
+                    nc.tensor.matmul_mx(acc[:], lhsT=slot_words[e, s].bitcast(FP8X4), lhsT_scale=slot_bytes[e, s],
+                                        rhs=w1_sb[e // 2][:, PASSES * (e % 2) + s, :].bitcast(FP4X4),
+                                        rhs_scale=w1_planes[e // 4][:, PASSES * (e % 4) + s, :],
+                                        start=(s == passes[0]), stop=(s == passes[-1]))
+            for e, acc in zip(pair, accs):
+                h_rows[e] = keep.tile([P, H], BF16, name=f"h_rows{e}", align_bytes=64)
+                dst = h_rows[e][:].rearrange("m (u p d) -> m u p d", u=2, d=2)
+                src = acc[:].rearrange("m (p u d) -> m u p d", u=2, d=2)
+                if e == E - 1:
+                    nc.vector.tensor_scalar_max(dst, src, 0.0)
+                else:
+                    nc.scalar.activation(dst, src, RELU)
 
         def quantise_hidden(group, number, move):
             n = len(group)
@@ -181,22 +183,18 @@ def tile_moe_ecr_mlp_relu_kernel(tc, xT, w1_words, w1_scales, w2_words, w2_scale
         gather(1, [(0,), (1,)], "_c")
         gather(1, [(2, 3)], "_d")
         gather(1, [(4, 5)], "_e")
-        first_layer(0, 0)
-        first_layer(1, 1)
+        first_layer((0, 1), (0, 1), (0, 1))
         gather(0, [(4, 5)], "_a")
-        first_layer(2, 2)
-        first_layer(3, 3)
+        first_layer((2, 3), (2, 3), (0, 1))
         gather(0, [(6, 7)], "_b")
         gather(1, [(6,), (7,)], "_d")
         quantise_hidden((0, 1), 2, nc.scalar.copy)
-        first_layer(4, 0)
-        first_layer(5, 1)
-        quantise_hidden((2, 3), 0, nc.scalar.copy)
-        first_layer(6, 3)
-        first_layer(7, 4)
+        quantise_hidden((2, 3), 4, nc.scalar.copy)
+        first_layer((4, 5), (0, 1), (1, 0))
+        first_layer((6, 7), (3, 2), (0, 1))
         quantise_hidden((4, 5), 3, nc.scalar.copy)
         quantise_hidden((6,), 1, nc.vector.tensor_copy)
-        quantise_hidden((7,), 2, nc.scalar.copy)
+        quantise_hidden((7,), 0, nc.scalar.copy)
         second_layer(0, (0, 1, 2, 3), 5, nc.scalar.copy)
         second_layer(0, (4, 5), 6, nc.vector.tensor_copy)
         second_layer(0, (6, 7), 7, nc.scalar.copy)
@@ -209,48 +207,39 @@ def tile_moe_ecr_mlp_relu_kernel(tc, xT, w1_words, w1_scales, w2_words, w2_scale
             nc.vector.tensor_tensor(term[:], y_sb[b][:].indirect(pos_sb[r][:, lo // 16:hi // 16]), gate_sb[:, r, lo:hi], MULT)
             return term
 
-        def turned_sum(b, choices, sums, backs):
-            width = T // len(sums)
-            per = width // P
+        def turned_sum(b, choices, parts, sum_banks, back_banks):
+            sums = [bank(number, [P, hi - lo]) for number, (lo, hi) in zip(sum_banks, parts)]
+            backs = [bank(number, [P, hi - lo]) for number, (lo, hi) in zip(back_banks, parts)]
             for r in range(choices):
-                cuts = len(sums) if r == choices - 1 else 1
-                for a in range(cuts):
-                    lo = T // cuts * a
-                    term = fetch(b, r, f"term{b}{r}{a}", lo, lo + T // cuts)
-                    for q in range(lo // P, (lo + T // cuts) // P):
-                        nc.tensor.matmul(sums[q // per][:, P * (q % per):P * (q % per + 1)],
-                                         lhsT=term[:, P * q - lo:P * (q + 1) - lo],
-                                         rhs=ident[:], is_transpose=True, start=(r == 0 and q % per == 0),
-                                         stop=(r == choices - 1 and q % per == per - 1))
-            for a, (summed, back) in enumerate(zip(sums, backs)):
-                summed_sb = keep.tile([P, width], F32, name=f"summed_sb{b}{a}", align_bytes=64)
+                closing = r == choices - 1
+                for cut_lo, cut_hi in (parts if closing else [(0, T)]):
+                    term = fetch(b, r, f"term{b}{r}_{cut_lo}", cut_lo, cut_hi)
+                    for summed, (lo, hi) in zip(sums, parts):
+                        for t0 in range(max(lo, cut_lo), min(hi, cut_hi), P):
+                            nc.tensor.matmul(summed[:, t0 - lo:t0 - lo + P], lhsT=term[:, t0 - cut_lo:t0 - cut_lo + P],
+                                             rhs=ident[:], is_transpose=True, start=(r == 0 and t0 == lo),
+                                             stop=(closing and t0 + P == hi))
+            for summed, back, (lo, hi) in zip(sums, backs, parts):
+                summed_sb = keep.tile([P, hi - lo], F32, name=f"summed_sb{b}_{lo}", align_bytes=64)
                 nc.scalar.copy(summed_sb[:], summed[:])
-                for q in range(per):
-                    cols = slice(P * q, P * (q + 1))
-                    nc.tensor.transpose(back[:, cols], summed_sb[:, cols], ident[:])
+                for c0 in range(0, hi - lo, P):
+                    nc.tensor.transpose(back[:, c0:c0 + P], summed_sb[:, c0:c0 + P], ident[:])
+            return backs
 
-        def copy_and_store(b, backs):
-            width = T // len(backs)
-            for a, back in enumerate(backs):
-                result = keep.tile([P, width], F32, name=f"result{b}{a}", align_bytes=64)
+        def copy_and_store(b, parts, backs):
+            for back, (lo, hi) in zip(backs, parts):
+                result = keep.tile([P, hi - lo], F32, name=f"result{b}_{lo}", align_bytes=64)
                 nc.scalar.copy(result[:], back[:])
-                nc.sync.dma_start(out[P * b:P * (b + 1), width * a:width * (a + 1)], result[:])
+                nc.sync.dma_start(out[P * b:P * (b + 1), lo:hi], result[:])
 
-        backs = [bank(1, [P, T])]
-        turned_sum(0, TOP, [bank(0, [P, T])], backs)
-        copy_and_store(0, backs)
+        whole = [(0, T)]
+        copy_and_store(0, whole, turned_sum(0, TOP, whole, [0], [1]))
+        partial = turned_sum(1, TOP - 1, whole, [2], [3])[0]
+        parts = [(0, 2 * P), (2 * P, 3 * P), (3 * P, T)]
+        copy_and_store(2, parts, turned_sum(2, TOP, parts, [4, 5, 0], [6, 7, 1]))
 
-        partial = bank(3, [P, T])
-        turned_sum(1, TOP - 1, [bank(2, [P, T])], [partial])
-
-        sums = [bank(4, [P, HALF]), bank(5, [P, HALF])]
-        backs = [bank(6, [P, HALF]), bank(7, [P, HALF])]
-        turned_sum(2, TOP, sums, backs)
-        copy_and_store(2, backs)
-
-        for a in range(2):
-            lo, hi = HALF * a, HALF * (a + 1)
-            last = fetch(1, TOP - 1, f"term1{a}0", lo, hi)
-            result = keep.tile([P, HALF], F32, name=f"result1{a}", align_bytes=64)
+        for r, (lo, hi) in enumerate([(0, 3 * P), (3 * P, T)]):
+            last = fetch(1, TOP - 1, f"term1{r}_0", lo, hi)
+            result = keep.tile([P, hi - lo], F32, name=f"result1_{lo}", align_bytes=64)
             nc.vector.tensor_tensor(result[:], partial[:, lo:hi], last[:], ADD)
             nc.sync.dma_start(out[P:2 * P, lo:hi], result[:])

@@ -26,6 +26,7 @@ MULT = mybir.AluOpType.mult
 ADD = mybir.AluOpType.add
 
 VECTOR_SHARE = 160
+SCALE_LOADS = [(0, 1), (2, 3), (4, 5, 6, 7)]
 HALF = T // 2
 
 
@@ -36,13 +37,13 @@ def tile_moe_ecr_mlp_relu_kernel(tc, xT, w1_words, w1_scales, w2_words, w2_scale
         keep = ctx.enter_context(tc.tile_pool(name="keep", bufs=1))
         psum = ctx.enter_context(tc.psum_pool(name="psum", bufs=1))
 
-        w1_planes = [keep.tile([P, 4 * PASSES, H], U8, name=f"w1_plane{a}", align_bytes=64) for a in range(2)]
+        w1_planes = {load: keep.tile([P, len(load) * PASSES, H], U8, name=f"w1_plane{load[0]}", align_bytes=64) for load in SCALE_LOADS}
         w2_plane = keep.tile([P, E, N], U8, name="w2_plane", align_bytes=64)
         tok_words = [keep.tile([P, T], U32, name=f"tok_words{s}", align_bytes=64) for s in range(PASSES)]
         tok_bytes = [keep.tile([P, T], U8, name=f"tok_bytes{s}", align_bytes=64) for s in range(PASSES)]
         y_sb = [keep.tile([P, S + PAD], F32, name=f"y_sb{b}", align_bytes=64) for b in range(BLOCKS)]
         ident = keep.tile([P, P], F32, name="ident", align_bytes=64)
-        for plane in w1_planes:
+        for plane in w1_planes.values():
             nc.vector.memset(plane[:].rearrange("p a i -> p (a i)").bitcast(I32), 0)
         nc.gpsimd.memset(y_sb[0][:, S:], 0.0)
         for s in range(PASSES):
@@ -69,26 +70,36 @@ def tile_moe_ecr_mlp_relu_kernel(tc, xT, w1_words, w1_scales, w2_words, w2_scale
                 nc.sync.dma_start(plane[r:P:32, :, :].bitcast(I32), src[r].bitcast(I32))
 
         w1_sb = {}
+        w1_scale = {}
 
-        def load_w1(a):
-            w1_sb[a] = keep.tile([P, 2 * PASSES, 2 * H], U8, name=f"w1_sb{a}", align_bytes=64)
-            src = w1_words[2 * a:2 * a + 2].rearrange("e s p b -> p (e s) b")
-            nc.sync.dma_start(w1_sb[a][:].bitcast(I32), src.bitcast(I32))
+        def load_w1(experts):
+            words = keep.tile([P, len(experts) * PASSES, 2 * H], U8, name=f"w1_sb{experts[0]}", align_bytes=64)
+            src = w1_words[experts[0]:experts[-1] + 1].rearrange("e s p b -> p (e s) b")
+            nc.sync.dma_start(words[:].bitcast(I32), src.bitcast(I32))
+            for g, e in enumerate(experts):
+                for s in range(PASSES):
+                    w1_sb[e, s] = words[:, PASSES * g + s, :]
 
-        def w1_rows(a):
-            return w1_scales[4 * a:4 * a + 4].rearrange("e s (q r) i -> r q (e s) i", r=4)
+        def load_w1_scales(experts):
+            src = w1_scales[experts[0]:experts[-1] + 1].rearrange("e s (q r) i -> r q (e s) i", r=4)
+            load_scales(w1_planes[experts], src)
+            for g, e in enumerate(experts):
+                for s in range(PASSES):
+                    w1_scale[e, s] = w1_planes[experts][:, PASSES * g + s, :]
 
         load_x(0, 0)
         load_x(0, 1)
         offs_sb = load_list("offs_sb", offs, S)
         load_x(1, 0)
         load_x(1, 1)
-        load_scales(w1_planes[0], w1_rows(0))
-        load_w1(0)
-        load_w1(1)
-        load_scales(w1_planes[1], w1_rows(1))
-        load_w1(2)
-        load_w1(3)
+        load_w1_scales((0, 1))
+        load_w1((0,))
+        load_w1((1,))
+        load_w1_scales((2, 3))
+        load_w1((2, 3))
+        load_w1_scales((4, 5, 6, 7))
+        load_w1((4, 5))
+        load_w1((6, 7))
         load_scales(w2_plane, w2_scales.rearrange("e s (q r) n -> r q (e s) n", r=4))
         w2_sb = keep.tile([P, E, 2 * N], U8, name="w2_sb", align_bytes=64)
         nc.sync.dma_start(w2_sb[:].bitcast(I32), w2_words.rearrange("e s p b -> p (e s) b").bitcast(I32))
@@ -136,8 +147,8 @@ def tile_moe_ecr_mlp_relu_kernel(tc, xT, w1_words, w1_scales, w2_words, w2_scale
             for s in passes:
                 for e, acc in zip(pair, accs):
                     nc.tensor.matmul_mx(acc[:], lhsT=slot_words[e, s].bitcast(FP8X4), lhsT_scale=slot_bytes[e, s],
-                                        rhs=w1_sb[e // 2][:, PASSES * (e % 2) + s, :].bitcast(FP4X4),
-                                        rhs_scale=w1_planes[e // 4][:, PASSES * (e % 4) + s, :],
+                                        rhs=w1_sb[e, s].bitcast(FP4X4),
+                                        rhs_scale=w1_scale[e, s],
                                         start=(s == passes[0]), stop=(s == passes[-1]))
             for e, acc in zip(pair, accs):
                 h_rows[e] = keep.tile([P, H], BF16, name=f"h_rows{e}", align_bytes=64)
@@ -183,7 +194,8 @@ def tile_moe_ecr_mlp_relu_kernel(tc, xT, w1_words, w1_scales, w2_words, w2_scale
         gather(1, [(0,), (1,)], "_c")
         gather(1, [(2, 3)], "_d")
         gather(1, [(4, 5)], "_e")
-        first_layer((0, 1), (0, 1), (0, 1))
+        first_layer((0,), (0,), (0, 1))
+        first_layer((1,), (1,), (0, 1))
         gather(0, [(4, 5)], "_a")
         first_layer((2, 3), (2, 3), (0, 1))
         gather(0, [(6, 7)], "_b")
@@ -235,10 +247,10 @@ def tile_moe_ecr_mlp_relu_kernel(tc, xT, w1_words, w1_scales, w2_words, w2_scale
         whole = [(0, T)]
         copy_and_store(0, whole, turned_sum(0, TOP, whole, [0], [1]))
         partial = turned_sum(1, TOP - 1, whole, [2], [3])[0]
-        parts = [(0, 2 * P), (2 * P, 3 * P), (3 * P, T)]
-        copy_and_store(2, parts, turned_sum(2, TOP, parts, [4, 5, 0], [6, 7, 1]))
+        halves = [(0, HALF), (HALF, T)]
+        copy_and_store(2, halves, turned_sum(2, TOP, halves, [4, 5], [6, 7]))
 
-        for r, (lo, hi) in enumerate([(0, 3 * P), (3 * P, T)]):
+        for r, (lo, hi) in enumerate(halves):
             last = fetch(1, TOP - 1, f"term1{r}_0", lo, hi)
             result = keep.tile([P, hi - lo], F32, name=f"result1_{lo}", align_bytes=64)
             nc.vector.tensor_tensor(result[:], partial[:, lo:hi], last[:], ADD)

from contextlib import ExitStack

import concourse.mybir as mybir
from concourse.masks import make_identity

K, T, E, C, H, N = 1024, 512, 8, 128, 512, 384
TOP, PAD = 3, 64
S = E * C
P = 128
PASSES = K // 512
BLOCKS = N // P

FLOPS = 2 * S * (K * H + H * N)
BYTES = 4 * K * T + E * (K * H + H * N) * 17 // 32 + 4 * TOP * T + 2 * P * (S + TOP * T) // 16 + 4 * N * T

F32 = mybir.dt.float32
BF16 = mybir.dt.bfloat16
I32 = mybir.dt.int32
U32 = mybir.dt.uint32
U16 = mybir.dt.uint16
U8 = mybir.dt.uint8
FP8X4 = mybir.dt.float8_e4m3fn_x4
FP4X4 = mybir.dt.float4_e2m1fn_x4
RELU = mybir.ActivationFunctionType.Relu
MULT = mybir.AluOpType.mult
ADD = mybir.AluOpType.add

VECTOR_SHARE = 160
SCALE_LOADS = [(0, 1), (2, 3), (4, 5, 6, 7)]
HALF = T // 2


def tile_moe_ecr_mlp_relu_kernel(tc, xT, w1_words, w1_scales, w2_words, w2_scales, gate, offs, pos1, pos2, pos3, out):
    nc = tc.nc
    with ExitStack() as ctx:
        lists = ctx.enter_context(tc.tile_pool(name="lists", bufs=1))
        keep = ctx.enter_context(tc.tile_pool(name="keep", bufs=1))
        psum = ctx.enter_context(tc.psum_pool(name="psum", bufs=1))

        w1_planes = {load: keep.tile([P, len(load) * PASSES, H], U8, name=f"w1_plane{load[0]}", align_bytes=64) for load in SCALE_LOADS}
        w2_plane = keep.tile([P, E, N], U8, name="w2_plane", align_bytes=64)
        tok_words = [keep.tile([P, T], U32, name=f"tok_words{s}", align_bytes=64) for s in range(PASSES)]
        tok_bytes = [keep.tile([P, T], U8, name=f"tok_bytes{s}", align_bytes=64) for s in range(PASSES)]
        y_sb = [keep.tile([P, S + PAD], F32, name=f"y_sb{b}", align_bytes=64) for b in range(BLOCKS)]
        ident = keep.tile([P, P], F32, name="ident", align_bytes=64)
        for plane in w1_planes.values():
            nc.vector.memset(plane[:].rearrange("p a i -> p (a i)").bitcast(I32), 0)
        nc.gpsimd.memset(y_sb[0][:, S:], 0.0)
        for s in range(PASSES):
            nc.gpsimd.memset(tok_bytes[s][:].bitcast(I32), 0)
        nc.gpsimd.memset(w2_plane[:].rearrange("p e n -> p (e n)").bitcast(I32), 0)
        make_identity(nc, ident[:])
        for b in range(1, BLOCKS):
            nc.scalar.activation(y_sb[b][:, S:], y_sb[0][:, S:], RELU)

        x_raw = {}

        def load_x(s, h):
            x_raw[s, h] = keep.tile([P, 4, HALF], F32, name=f"x_raw{s}{h}", align_bytes=64)
            rows = xT[512 * s:512 * (s + 1), HALF * h:HALF * (h + 1)]
            nc.sync.dma_start(x_raw[s, h][:], rows.rearrange("(p j) t -> p j t", j=4))

        def load_list(name, src, entries):
            t = lists.tile([P, entries // 16], U16, name=name)
            nc.sync.dma_start(t[:], src)
            return t

        def load_scales(plane, src):
            for r in range(4):
                nc.sync.dma_start(plane[r:P:32, :, :].bitcast(I32), src[r].bitcast(I32))

        w1_sb = {}
        w1_scale = {}

        def load_w1(experts):
            words = keep.tile([P, len(experts) * PASSES, 2 * H], U8, name=f"w1_sb{experts[0]}", align_bytes=64)
            src = w1_words[experts[0]:experts[-1] + 1].rearrange("e s p b -> p (e s) b")
            nc.sync.dma_start(words[:].bitcast(I32), src.bitcast(I32))
            for g, e in enumerate(experts):
                for s in range(PASSES):
                    w1_sb[e, s] = words[:, PASSES * g + s, :]

        def load_w1_scales(experts):
            src = w1_scales[experts[0]:experts[-1] + 1].rearrange("e s (q r) i -> r q (e s) i", r=4)
            load_scales(w1_planes[experts], src)
            for g, e in enumerate(experts):
                for s in range(PASSES):
                    w1_scale[e, s] = w1_planes[experts][:, PASSES * g + s, :]

        load_x(0, 0)
        load_x(0, 1)
        offs_sb = load_list("offs_sb", offs, S)
        load_x(1, 0)
        load_x(1, 1)
        load_w1_scales((0, 1))
        load_w1((0,))
        load_w1((1,))
        load_w1_scales((2, 3))
        load_w1((2, 3))
        load_w1_scales((4, 5, 6, 7))
        load_w1((4, 5))
        load_w1((6, 7))
        load_scales(w2_plane, w2_scales.rearrange("e s (q r) n -> r q (e s) n", r=4))
        w2_sb = keep.tile([P, E, 2 * N], U8, name="w2_sb", align_bytes=64)
        nc.sync.dma_start(w2_sb[:].bitcast(I32), w2_words.rearrange("e s p b -> p (e s) b").bitcast(I32))
        pos_sb = [load_list(f"pos_sb{r}", src, T) for r, src in enumerate((pos1, pos2, pos3))]
        gate_sb = keep.tile([P, TOP, T], F32, name="gate_sb", align_bytes=64)
        nc.sync.dma_start(gate_sb[:], gate[:, 0:P, :].rearrange("r p t -> p r t"))

        def quantise_tokens(s, h, vector_tokens):
            x_bf = keep.tile([P, HALF, 4], BF16, name=f"x_bf{s}{h}", align_bytes=64)
            for move, lo, hi in ((nc.vector.tensor_copy, 0, vector_tokens), (nc.scalar.copy, vector_tokens, HALF)):
                if lo < hi:
                    move(x_bf[:, lo:hi, :].rearrange("p (c i) j -> p c j i", i=4),
                         x_raw[s, h][:, :, lo:hi].rearrange("p j (c i) -> p c j i", i=4))
            cols = slice(HALF * h, HALF * (h + 1))
            nc.vector.quantize_mx(out=tok_words[s][:, cols].bitcast(FP8X4), scales=tok_bytes[s][:, cols],
                                  in_=x_bf[:].rearrange("p t j -> p (t j)"))

        slot_words = {}
        slot_bytes = {}
        h_words = {}
        h_bytes = {}

        def gather(s, cuts, tag):
            first = cuts[0][0]
            width = C * sum(len(cut) for cut in cuts)
            words = keep.tile([P, width], U32, name="slot_words" + tag, align_bytes=64)
            scale = keep.tile([P, width], U8, name="slot_bytes" + tag, align_bytes=64)
            for cut in cuts:
                idx = offs_sb[:, C * cut[0] // 16:C * (cut[-1] + 1) // 16]
                cols = slice(C * (cut[0] - first), C * (cut[-1] + 1 - first))
                nc.vector.tensor_copy(words[:, cols], tok_words[s][:].indirect(idx))
                nc.vector.tensor_copy(scale[:, cols], tok_bytes[s][:].indirect(idx))
                for e in cut:
                    cols = slice(C * (e - first), C * (e + 1 - first))
                    slot_words[e, s] = words[:, cols]
                    slot_bytes[e, s] = scale[:, cols]

        def bank(number, shape):
            return psum.tile(shape, F32, name=f"bank{number}")

        h_rows = {}

        def first_layer(pair, numbers, passes):
            accs = [bank(number, [P, H]) for number in numbers]
            for s in passes:
                for e, acc in zip(pair, accs):
                    nc.tensor.matmul_mx(acc[:], lhsT=slot_words[e, s].bitcast(FP8X4), lhsT_scale=slot_bytes[e, s],
                                        rhs=w1_sb[e, s].bitcast(FP4X4),
                                        rhs_scale=w1_scale[e, s],
                                        start=(s == passes[0]), stop=(s == passes[-1]))
            for e, acc in zip(pair, accs):
                h_rows[e] = keep.tile([P, H], BF16, name=f"h_rows{e}", align_bytes=64)
                dst = h_rows[e][:].rearrange("m (u p d) -> m u p d", u=2, d=2)
                src = acc[:].rearrange("m (p u d) -> m u p d", u=2, d=2)
                if e == E - 1:
                    nc.vector.tensor_scalar_max(dst, src, 0.0)
                else:
                    nc.scalar.activation(dst, src, RELU)

        def quantise_hidden(group, number, move):
            n = len(group)
            turned = bank(number, [P, n, 2, C])
            for g, e in enumerate(group):
                pairs = h_rows[e][:].bitcast(F32)
                for u in range(2):
                    nc.tensor.transpose(turned[:, g, u, :], pairs[:, P * u:P * (u + 1)], ident[:])
            h_bf = keep.tile([P, 4 * C * n], BF16, name=f"h_bf{group[0]}", align_bytes=64)
            move(h_bf[:].bitcast(F32).rearrange("p (g m u) -> p g m u", g=n, u=2),
                 turned[:].rearrange("p g u m -> p g m u"))
            words = keep.tile([P, C * n], U32, name=f"h_words{group[0]}", align_bytes=64)
            scale = keep.tile([P, C * n], U8, name=f"h_bytes{group[0]}", align_bytes=64)
            nc.vector.quantize_mx(out=words[:].bitcast(FP8X4), scales=scale[:], in_=h_bf[:])
            for g, e in enumerate(group):
                h_words[e] = words[:, C * g:C * (g + 1)]
                h_bytes[e] = scale[:, C * g:C * (g + 1)]

        def second_layer(b, experts, number, move):
            y_ps = bank(number, [P, C * len(experts)])
            for g, e in enumerate(experts):
                nc.tensor.matmul_mx(y_ps[:, C * g:C * (g + 1)],
                                    lhsT=w2_sb[:, e, 2 * P * b:2 * P * (b + 1)].bitcast(FP4X4),
                                    lhsT_scale=w2_plane[:, e, P * b:P * (b + 1)],
                                    rhs=h_words[e].bitcast(FP8X4), rhs_scale=h_bytes[e], start=True, stop=True)
            move(y_sb[b][:, C * experts[0]:C * (experts[-1] + 1)], y_ps[:])

        quantise_tokens(0, 0, HALF)
        quantise_tokens(0, 1, VECTOR_SHARE)
        gather(0, [(0, 1)], "_a")
        gather(0, [(2, 3)], "_b")
        for h in range(2):
            quantise_tokens(1, h, 0)
        gather(1, [(0,), (1,)], "_c")
        gather(1, [(2, 3)], "_d")
        gather(1, [(4, 5)], "_e")
        first_layer((0,), (0,), (0, 1))
        first_layer((1,), (1,), (0, 1))
        gather(0, [(4, 5)], "_a")
        first_layer((2, 3), (2, 3), (0, 1))
        gather(0, [(6, 7)], "_b")
        gather(1, [(6,), (7,)], "_d")
        quantise_hidden((0, 1), 2, nc.scalar.copy)
        quantise_hidden((2, 3), 4, nc.scalar.copy)
        first_layer((4, 5), (0, 1), (1, 0))
        first_layer((6, 7), (3, 2), (0, 1))
        quantise_hidden((4, 5), 3, nc.scalar.copy)
        quantise_hidden((6,), 1, nc.vector.tensor_copy)
        quantise_hidden((7,), 0, nc.scalar.copy)
        second_layer(0, (0, 1, 2, 3), 5, nc.scalar.copy)
        second_layer(0, (4, 5), 6, nc.vector.tensor_copy)
        second_layer(0, (6, 7), 7, nc.scalar.copy)
        for b in range(1, BLOCKS):
            second_layer(b, (0, 1, 2, 3), 7, nc.scalar.copy)
            second_layer(b, (4, 5, 6, 7), 5 if b == 1 else 6, nc.scalar.copy)

        def fetch(b, r, tag, lo=0, hi=T):
            term = keep.tile([P, hi - lo], F32, name=tag, align_bytes=64)
            nc.vector.tensor_tensor(term[:], y_sb[b][:].indirect(pos_sb[r][:, lo // 16:hi // 16]), gate_sb[:, r, lo:hi], MULT)
            return term

        def turned_sum(b, choices, parts, sum_banks, back_banks):
            sums = [bank(number, [P, hi - lo]) for number, (lo, hi) in zip(sum_banks, parts)]
            backs = [bank(number, [P, hi - lo]) for number, (lo, hi) in zip(back_banks, parts)]
            for r in range(choices):
                closing = r == choices - 1
                for cut_lo, cut_hi in (parts if closing else [(0, T)]):
                    term = fetch(b, r, f"term{b}{r}_{cut_lo}", cut_lo, cut_hi)
                    for summed, (lo, hi) in zip(sums, parts):
                        for t0 in range(max(lo, cut_lo), min(hi, cut_hi), P):
                            nc.tensor.matmul(summed[:, t0 - lo:t0 - lo + P], lhsT=term[:, t0 - cut_lo:t0 - cut_lo + P],
                                             rhs=ident[:], is_transpose=True, start=(r == 0 and t0 == lo),
                                             stop=(closing and t0 + P == hi))
            for summed, back, (lo, hi) in zip(sums, backs, parts):
                summed_sb = keep.tile([P, hi - lo], F32, name=f"summed_sb{b}_{lo}", align_bytes=64)
                nc.scalar.copy(summed_sb[:], summed[:])
                for c0 in range(0, hi - lo, P):
                    nc.tensor.transpose(back[:, c0:c0 + P], summed_sb[:, c0:c0 + P], ident[:])
            return backs

        def copy_and_store(b, parts, backs):
            for back, (lo, hi) in zip(backs, parts):
                result = keep.tile([P, hi - lo], F32, name=f"result{b}_{lo}", align_bytes=64)
                nc.scalar.copy(result[:], back[:])
                nc.sync.dma_start(out[P * b:P * (b + 1), lo:hi], result[:])

        whole = [(0, T)]
        copy_and_store(0, whole, turned_sum(0, TOP, whole, [0], [1]))
        partial = turned_sum(1, TOP - 1, whole, [2], [3])[0]
        halves = [(0, HALF), (HALF, T)]
        copy_and_store(2, halves, turned_sum(2, TOP, halves, [4, 5], [6, 7]))

        for r, (lo, hi) in enumerate(halves):
            last = fetch(1, TOP - 1, f"term1{r}_0", lo, hi)
            result = keep.tile([P, hi - lo], F32, name=f"result1_{lo}", align_bytes=64)
            nc.vector.tensor_tensor(result[:], partial[:, lo:hi], last[:], ADD)
            nc.sync.dma_start(out[P:2 * P, lo:hi], result[:])
